import numpy as np
import ml_dtypes


def mxq(x, axis, fmt="e4m3"):
    dtype, down = {"e4m3": (ml_dtypes.float8_e4m3fn, 7), "e5m2": (ml_dtypes.float8_e5m2, 14)}[fmt]
    v = np.moveaxis(np.asarray(x, np.float32).astype(ml_dtypes.bfloat16).astype(np.float64), axis, -1)
    blocks = v.reshape(v.shape[:-1] + (-1, 32))
    amax = np.abs(blocks).max(-1, keepdims=True)
    byte = np.maximum(np.where(amax > 0, np.frexp(amax)[1] - 1 + 127, 0) - down, 1)
    scale = np.exp2(byte - 127.0)
    codes = (blocks / scale).astype(np.float32).astype(dtype).astype(np.float64)
    return np.moveaxis((codes * scale).reshape(v.shape), -1, axis)


WIDE = False


def mx_kscale(k):
    if not WIDE:
        return np.ones(k)
    levels = np.array([10, -10, 5, -5, 0])
    if k % 512:
        return np.exp2(np.random.permutation(np.resize(levels, k // 32))).repeat(32)
    a = np.empty((k // 512, 16))
    for p in range(k // 512):
        a[p, :8] = np.random.permutation(np.resize(levels, 8))
        for g in range(8):
            far = levels[np.abs(levels - a[p, g]) >= 10]
            a[p, g + 8] = far[np.random.randint(len(far))]
    return np.exp2(a.ravel()).repeat(32)


def f64(x):
    return np.asarray(x).astype(np.float64)


def striped(idx):
    return np.tile(idx.reshape(-1, 16).T, (8, 1)).astype(np.uint16)


def unstriped(offs):
    return offs[:16].T.reshape(-1).astype(np.int64)


def relu2(v):
    return np.maximum(v, 0.0) ** 2


K, T, E, C, H, N = 1024, 1536, 4, 256, 512, 256


def by_expert(wq, xq):
    return np.concatenate([wq[e].T @ xq[:, e * C:(e + 1) * C] for e in range(E)], axis=1)


def setup_inputs():
    n = np.random.standard_normal
    s = mx_kscale(K)[:, None]
    u = mx_kscale(H)
    return {
        "xT": (n((K, T)) * s).astype(np.float32),
        "w1": (n((E, K, H)) / np.sqrt(K) / s[None] * u[None, None, :]).astype(np.float32),
        "w2": (n((E, H, N)) / np.sqrt(H) / u[None, :, None] ** 2).astype(np.float32),
        "gate": np.tile(np.random.uniform(0.2, 1.0, E * C), (N, 1)).astype(np.float32),
        "offs": striped(np.random.permutation(T)[:E * C]),
    }


def reference(xT, w1, w2, gate, offs):
    idx = unstriped(offs)
    xq = mxq(f64(xT)[:, idx], 0, "e4m3")
    h = relu2(by_expert(mxq(f64(w1), 1, "e4m3"), xq))
    y = by_expert(mxq(f64(w2), 1, "e4m3"), mxq(h, 0, "e4m3"))
    out = np.zeros((N, T))
    out[:, idx] = f64(gate) * y
    return out

@@ -1,0 +1,206 @@
+from contextlib import ExitStack
+
+import concourse.mybir as mybir
+
+K, T, E, C, H, N = 1024, 1536, 4, 256, 512, 256
+FLOPS = 2 * E * C * (K * H + H * N)
+F32 = mybir.dt.float32
+BF16 = mybir.dt.bfloat16
+U32 = mybir.dt.uint32
+U16 = mybir.dt.uint16
+U8 = mybir.dt.uint8
+FP8X4 = mybir.dt.float8_e4m3fn_x4
+MULT = mybir.AluOpType.mult
+ADD = mybir.AluOpType.add
+RELU = mybir.ActivationFunctionType.Relu
+SQUARE = mybir.ActivationFunctionType.Square
+P = 128
+CX = [128,128,128,128,128,128]
+CW1 = [[0,32],[0,32],[0,32],[0,32],[0,32],[0,32],[0,64],[0,64]]
+CW2 = [[0,128],[0,192],[0,128],[64,192]]
+RL = ["S","S","S","S","S","S","S","S"]
+SQ = ["S","S","S","S","S","S","S","S"]
+EV = ["S","S","S","S"]
+GS = [[1,3],[1,3],[2,2]]
+HQ = 1
+TEXT = """lst x00 x01 x02 x10 x11 x12 w1_00 w1_01 w2_0 w1_10 w1_11 w1_20 ms0 ms1 cxV00 cxS00 qx00 cxV01 cxS01 qx01 cxV02 cxS02 qx02 cxV10 cxS10 qx10 cxV11 cxS11 qx11 cxV12 cxS12 qx12 c1G00 c1S00 w1_21 c1G01 c1S01 w1_30 q100 q101 gw00 gw10 gb0 m100 r00 s00 qh00 m101 r01 s01 qh01 c2G0 c2S0 q20 m20 y0 c1G10 c1S10 w1_31 w2_1 w2_2 c1G11 c1S11 q110 q111 gw01 gw11 gb1 m110 r10 s10 qh10 m111 r11 s11 qh11 c2G1 c2S1 w2_3 gate q21 m21 y1 sc00 sc01 c1G20 c1S20 c1G21 c1S21 q120 q121 m120 r20 s20 qh20 m121 r21 s21 qh21 c2G2 c2S2 q22 m22 y2 sc10 sc11 c1G30 c1S30 c1G31 c1S31 q130 q131 m130 r30 s30 qh30 m131 r31 s31 qh31 c2V3 c2G3 q23 m23 y3 sc20 sc21 sc30 sc31 st0 st1"""
+
+
+def tile_routed_moe_kernel(tc, xT, w1, w2, gate, offs, out):
+    nc = tc.nc
+    with ExitStack() as ctx:
+        keep = ctx.enter_context(tc.tile_pool(name="keep", bufs=1))
+        rxp = ctx.enter_context(tc.tile_pool(name="rxp", bufs=6))
+        rwp = ctx.enter_context(tc.tile_pool(name="rwp", bufs=5))
+        r2p = ctx.enter_context(tc.tile_pool(name="r2p", bufs=2))
+        xbp = ctx.enter_context(tc.tile_pool(name="xbp", bufs=2))
+        wbp = ctx.enter_context(tc.tile_pool(name="wbp", bufs=4))
+        hbp = ctx.enter_context(tc.tile_pool(name="hbp", bufs=4))
+        hp = ctx.enter_context(tc.tile_pool(name="hp", bufs=3))
+        psum_h = ctx.enter_context(tc.psum_pool(name="psum_h", bufs=4))
+        psum_y = ctx.enter_context(tc.psum_pool(name="psum_y", bufs=3))
+        xv = xT.rearrange("(a p j) n -> a p j n", p=P, j=4)
+        tl = {}
+        lst = keep.tile([P, E * C // 16], U16, name="lst")
+        xw = [keep.tile([P, T], U32, name=f"xw{a}", align_bytes=64) for a in range(2)]
+        xs = keep.tile([P, T], U8, name="xs", align_bytes=64)
+        nc.gpsimd.memset(xs[:], 0)
+        win = [keep.tile([P, T], F32, name=f"win{b}", align_bytes=64) for b in range(2)]
+        xg = keep.tile([P, 2, E * C], U32, name="xg", align_bytes=64)
+        xgs = keep.tile([P, E * C], U8, name="xgs", align_bytes=64)
+        gate_sb = keep.tile([P, 2, E * C], F32, name="gate_sb")
+
+        def get(key, pool, shape, dt, tag):
+            if key not in tl:
+                if pool is psum_h or pool is psum_y:
+                    tl[key] = pool.tile(shape, dt, name=tag)
+                else:
+                    tl[key] = pool.tile(shape, dt, name=tag, align_bytes=64)
+            return tl[key]
+
+        def cast(eng, dst, src):
+            if eng == "V":
+                nc.vector.tensor_copy(dst, src)
+            elif eng == "S":
+                nc.scalar.copy(dst, src)
+            else:
+                nc.gpsimd.tensor_scalar(dst, src, 1.0, 0.0, MULT, ADD)
+
+        def cols(eng, g, raw, c0, c1):
+            d, s = g[:, c0:c1, :], raw[:, :, c0:c1]
+            if eng == "G":
+                cast(eng, d, s.rearrange("p j c -> p c j"))
+            else:
+                cast(eng, d.rearrange("p (c i) j -> p c j i", i=4), s.rearrange("p j (c i) -> p c j i", i=4))
+
+        def w1cols(eng, g, raw, m0, m1):
+            d = g[:].rearrange("p (t m) j -> p t m j", t=4)[:, :, m0:m1]
+            s = raw[:].rearrange("p j (m t) -> p t m j", t=4)[:, :, m0:m1]
+            if eng == "G":
+                cast(eng, d, s)
+            else:
+                cast(eng, d.rearrange("p t m j -> p m j t"), s.rearrange("p t m j -> p m j t"))
+
+        def psum_op(eng, dst, src, func):
+            if eng == "S":
+                nc.scalar.activation(dst, src, func)
+            elif func == RELU:
+                nc.vector.tensor_scalar(dst, src, 0.0, None, mybir.AluOpType.max)
+            else:
+                nc.vector.tensor_tensor(dst, src, src, MULT)
+
+        for i in TEXT.split(" "):
+            if i == "lst":
+                nc.sync.dma_start(lst[:], offs)
+            elif i.startswith("x"):
+                a, c = int(i[1]), int(i[2])
+                t = get("x" + i[1:], rxp, [P, 4, 512], F32, "raw")
+                nc.sync.dma_start(t[:], xv[a][:, :, c * 512 : (c + 1) * 512])
+            elif i.startswith("w1_"):
+                e, a = int(i[3]), int(i[4])
+                t = get("w1" + i[3:], rwp, [P, 4, 512], F32, "raw")
+                nc.sync.dma_start(t[:], w1[e].rearrange("(a p j) h -> a p j h", p=P, j=4)[a])
+            elif i.startswith("w2_"):
+                t = get("w2" + i[3:], r2p, [P, 4, N], F32, "w2r")
+                nc.sync.dma_start(t[:], w2[int(i[3])].rearrange("(p j) n -> p j n", j=4))
+            elif i == "gate":
+                nc.sync.dma_start(gate_sb[:], gate.rearrange("(b p) j -> p b j", p=P))
+            elif i.startswith("ms"):
+                nc.vector.memset(win[int(i[2])][:], 0.0)
+            elif i.startswith("cx"):
+                a, c = int(i[3]), int(i[4])
+                g = get("xb" + i[3:], xbp, [P, 512, 4], BF16, "xb")
+                v = CX[3 * a + c]
+                cols(i[2], g, tl["x" + i[3:]], *((0, v) if i[2] == "V" else (v, 512)))
+            elif i.startswith("qx"):
+                a, c = int(i[2]), int(i[3])
+                s = slice(c * 512, (c + 1) * 512)
+                nc.vector.quantize_mx(out=xw[a][:, s].bitcast(FP8X4), scales=xs[4 * a : P, s], in_=tl["xb" + i[2:]][:].rearrange("p w j -> p (w j)"))
+            elif i.startswith("gw"):
+                a, s = int(i[2]), int(i[3])
+                j0 = 256 * sum(GS[a][:s])
+                j1 = j0 + 256 * GS[a][s]
+                nc.vector.tensor_copy(xg[:, a, j0:j1], xw[a][:].indirect(lst[:, j0 // 16 : j1 // 16]))
+            elif i.startswith("gb"):
+                s = int(i[2])
+                j0 = 256 * sum(GS[2][:s])
+                j1 = j0 + 256 * GS[2][s]
+                nc.vector.tensor_copy(xgs[:, j0:j1], xs[:].indirect(lst[:, j0 // 16 : j1 // 16]))
+            elif i.startswith("c1"):
+                e, a = int(i[3]), int(i[4])
+                g = get("wb" + i[3:], wbp, [P, 512, 4], BF16, "wb")
+                v, gp = CW1[2 * e + a]
+                w1cols(i[2], g, tl["w1" + i[3:]], *{"V": (0, v), "G": (v, v + gp), "S": (v + gp, 128)}[i[2]])
+            elif i.startswith("q1"):
+                e, a = int(i[2]), int(i[3])
+                wc = get("w1c%d" % e, keep, [P, 2, H], U32, "w1c%d" % e)
+                ws = get("w1s%d" % e, keep, [P, 2, H], U8, "w1s%d" % e)
+                nc.vector.quantize_mx(out=wc[:, a, :].bitcast(FP8X4), scales=ws[:, a, :], in_=tl["wb" + i[2:]][:].rearrange("p w j -> p (w j)"))
+            elif i.startswith("c2"):
+                e = int(i[3])
+                g = get("w2b" + i[3], hp, [P, N, 4], BF16, "w2b")
+                v, gp = CW2[e]
+                cols(i[2], g, tl["w2" + i[3]], *{"V": (0, v), "G": (v, v + gp), "S": (v + gp, N)}[i[2]])
+            elif i.startswith("q2"):
+                e = int(i[2])
+                wc = get("w2c%d" % e, keep, [P, N], U32, "w2c%d" % e)
+                ws = get("w2s%d" % e, keep, [P, N], U8, "w2s%d" % e)
+                nc.vector.quantize_mx(out=wc[:].bitcast(FP8X4), scales=ws[:], in_=tl["w2b" + i[2]][:].rearrange("p w j -> p (w j)"))
+            elif i.startswith("m1"):
+                e, s = int(i[2]), int(i[3])
+                ph = get("ph" + i[2:], psum_h, [P, 4, 128], F32, "ph")
+                sl = slice(C * e + 128 * s, C * e + 128 * (s + 1))
+                for t in range(4):
+                    for a in range(2):
+                        nc.tensor.matmul_mx(
+                            out=ph[:, t, :],
+                            lhsT=tl["w1c%d" % e][:, a, P * t : P * (t + 1)].bitcast(FP8X4),
+                            lhsT_scale=tl["w1s%d" % e][:, a, P * t : P * (t + 1)],
+                            rhs=xg[:, a, sl].bitcast(FP8X4),
+                            rhs_scale=xgs[4 * a : P, sl],
+                            start=(a == 0),
+                            stop=(a == 1),
+                        )
+            elif i.startswith("r"):
+                r = get("r" + i[1:], hp, [P, 128, 4], F32, "r")
+                psum_op(RL[2 * int(i[1]) + int(i[2])], r[:], tl["ph" + i[1:]][:].rearrange("p t n -> p n t"), RELU)
+            elif i.startswith("qh"):
+                e = int(i[2])
+                hc = get("hc%d" % e, hp, [P, C], U32, "hc")
+                hs = get("hs%d" % e, hp, [P, C], U8, "hs")
+                s0, s1 = (0, C) if not HQ else (128 * int(i[3]), 128 * int(i[3]) + 128)
+                nc.vector.quantize_mx(out=hc[:, s0:s1].bitcast(FP8X4), scales=hs[:, s0:s1], in_=tl["hb%d" % e][:, s0:s1, :].rearrange("p w j -> p (w j)"))
+            elif i.startswith("m2"):
+                e = int(i[2])
+                y = get("y%d" % e, psum_y, [P, 2, C], F32, "y")
+                for b in range(2):
+                    nc.tensor.matmul_mx(
+                        out=y[:, b, :],
+                        lhsT=tl["w2c%d" % e][:, P * b : P * (b + 1)].bitcast(FP8X4),
+                        lhsT_scale=tl["w2s%d" % e][:, P * b : P * (b + 1)],
+                        rhs=tl["hc%d" % e][:].bitcast(FP8X4),
+                        rhs_scale=tl["hs%d" % e][:],
+                        start=True,
+                        stop=True,
+                    )
+            elif i.startswith("y"):
+                e = int(i[1])
+                ys = get("ys%d" % e, hp, [P, 2, C], F32, "ys")
+                if EV[e] == "S":
+                    nc.scalar.copy(ys[:], tl["y%d" % e][:])
+                else:
+                    nc.vector.tensor_tensor(ys[:], tl["y%d" % e][:], gate_sb[:, :, C * e : C * (e + 1)], MULT)
+            elif i.startswith("sc"):
+                e, b = int(i[2]), int(i[3])
+                w = win[b][:].indirect(lst[:, 16 * e : 16 * (e + 1)])
+                if EV[e] == "S":
+                    nc.vector.tensor_tensor(w, tl["ys%d" % e][:, b, :], gate_sb[:, b, C * e : C * (e + 1)], MULT)
+                else:
+                    nc.vector.tensor_copy(w, tl["ys%d" % e][:, b, :])
+            elif i.startswith("st"):
+                b = int(i[2])
+                nc.sync.dma_start(out[P * b : P * (b + 1), :], win[b][:])
+            elif i.startswith("s"):
+                e, s = int(i[1]), int(i[2])
+                hb = get("hb%d" % e, hbp, [P, C, 4], BF16, "hb")
+                psum_op(SQ[2 * e + s], hb[:, 128 * s : 128 * (s + 1), :], tl["r" + i[1:]][:], SQUARE)

@@ -15,28 +15,22 @@ ADD = mybir.AluOpType.add
 RELU = mybir.ActivationFunctionType.Relu
 SQUARE = mybir.ActivationFunctionType.Square
 P = 128
-CX = [128,128,128,128,128,128]
-CW1 = [[0,32],[0,32],[0,32],[0,32],[0,32],[0,32],[0,64],[0,64]]
-CW2 = [[0,128],[0,192],[0,128],[64,192]]
-RL = ["S","S","S","S","S","S","S","S"]
-SQ = ["S","S","S","S","S","S","S","S"]
-EV = ["S","S","S","S"]
-GS = [[1,3],[1,3],[2,2]]
-HQ = 1
-TEXT = """lst x00 x01 x02 x10 x11 x12 w1_00 w1_01 w2_0 w1_10 w1_11 w1_20 ms0 ms1 cxV00 cxS00 qx00 cxV01 cxS01 qx01 cxV02 cxS02 qx02 cxV10 cxS10 qx10 cxV11 cxS11 qx11 cxV12 cxS12 qx12 c1G00 c1S00 w1_21 c1G01 c1S01 w1_30 q100 q101 gw00 gw10 gb0 m100 r00 s00 qh00 m101 r01 s01 qh01 c2G0 c2S0 q20 m20 y0 c1G10 c1S10 w1_31 w2_1 w2_2 c1G11 c1S11 q110 q111 gw01 gw11 gb1 m110 r10 s10 qh10 m111 r11 s11 qh11 c2G1 c2S1 w2_3 gate q21 m21 y1 sc00 sc01 c1G20 c1S20 c1G21 c1S21 q120 q121 m120 r20 s20 qh20 m121 r21 s21 qh21 c2G2 c2S2 q22 m22 y2 sc10 sc11 c1G30 c1S30 c1G31 c1S31 q130 q131 m130 r30 s30 qh30 m131 r31 s31 qh31 c2V3 c2G3 q23 m23 y3 sc20 sc21 sc30 sc31 st0 st1"""
+CFG = {"xch":[1,1,1],"xv":192,"q2":[[0,1],[2,3]],"w2g":0.5,"gs":[[4],[4],[4]],"qm":[1,2,2,2],"w1":[[0,0],[0,64],[0,64],[48,32]],"rl":["V","S","S","S"],"sqm":[2,1,1,2],"sqe":["V","S","S","S"],"ev":"S","scg":[[0],[1],[2],[3]],"ld":"D","ord":1}
+TEXT = """lst x00 x01 x02 x10 x11 x12 w1_00 w1_01 w2_0 w1_10 w1_11 gate w1_20 w1_21 w1_30 w1_31 w2_1 ms0 ms1 cxV00 cxS00 qx00 cxV01 cxS01 qx01 cxV02 cxS02 qx02 gw00 cxV10 cxS10 qx10 cxV11 cxS11 qx11 cxV12 cxS12 qx12 c1S00 c1S01 q100 gw10 gb0 m100 r00 m101 r01 s00 s01 qh0 c2G0 c2S0 q20 m20 y0 c1G10 c1S10 c1G11 c1S11 q110 q111 sc00 sc01 m110 r10 m111 r11 s10 qh1 m21 y1 c1G20 c1S20 c1G21 c1S21 q120 q121 sc10 sc11 m120 r20 m121 r21 s20 qh2 c2G1 c2S1 q21 m22 y2 c1V30 c1G30 c1S30 c1V31 c1G31 c1S31 q130 q131 sc20 sc21 m130 r30 m131 r31 s30 s31 qh3 m23 y3 sc30 sc31 st0 st1"""
 
 
 def tile_routed_moe_kernel(tc, xT, w1, w2, gate, offs, out):
     nc = tc.nc
     with ExitStack() as ctx:
         keep = ctx.enter_context(tc.tile_pool(name="keep", bufs=1))
-        rxp = ctx.enter_context(tc.tile_pool(name="rxp", bufs=6))
-        rwp = ctx.enter_context(tc.tile_pool(name="rwp", bufs=5))
-        r2p = ctx.enter_context(tc.tile_pool(name="r2p", bufs=2))
-        xbp = ctx.enter_context(tc.tile_pool(name="xbp", bufs=2))
-        wbp = ctx.enter_context(tc.tile_pool(name="wbp", bufs=4))
-        hbp = ctx.enter_context(tc.tile_pool(name="hbp", bufs=4))
-        hp = ctx.enter_context(tc.tile_pool(name="hp", bufs=3))
+        p_raw = ctx.enter_context(tc.tile_pool(name="p_raw", bufs=11))
+        p_xb = ctx.enter_context(tc.tile_pool(name="p_xb", bufs=2))
+        p_wb = ctx.enter_context(tc.tile_pool(name="p_wb", bufs=2))
+        p_w2b = ctx.enter_context(tc.tile_pool(name="p_w2b", bufs=2))
+        p_r = ctx.enter_context(tc.tile_pool(name="p_r", bufs=2))
+        p_hb = ctx.enter_context(tc.tile_pool(name="p_hb", bufs=2))
+        p_hc = ctx.enter_context(tc.tile_pool(name="p_hc", bufs=3))
+        p_ys = ctx.enter_context(tc.tile_pool(name="p_ys", bufs=2))
         psum_h = ctx.enter_context(tc.psum_pool(name="psum_h", bufs=4))
         psum_y = ctx.enter_context(tc.psum_pool(name="psum_y", bufs=3))
         xv = xT.rearrange("(a p j) n -> a p j n", p=P, j=4)
@@ -49,6 +43,9 @@ def tile_routed_moe_kernel(tc, xT, w1, w2, gate, offs, out):
         xg = keep.tile([P, 2, E * C], U32, name="xg", align_bytes=64)
         xgs = keep.tile([P, E * C], U8, name="xgs", align_bytes=64)
         gate_sb = keep.tile([P, 2, E * C], F32, name="gate_sb")
+        XCH, XV, GS = CFG["xch"], CFG["xv"], CFG["gs"]
+        w2c = keep.tile([P, E, N], U32, name="w2c", align_bytes=64)
+        w2s = keep.tile([P, E, N], U8, name="w2s", align_bytes=64)
 
         def get(key, pool, shape, dt, tag):
             if key not in tl:
@@ -66,55 +63,59 @@ def tile_routed_moe_kernel(tc, xT, w1, w2, gate, offs, out):
             else:
                 nc.gpsimd.tensor_scalar(dst, src, 1.0, 0.0, MULT, ADD)
 
-        def cols(eng, g, raw, c0, c1):
-            d, s = g[:, c0:c1, :], raw[:, :, c0:c1]
+        def cols(eng, d, s):
             if eng == "G":
                 cast(eng, d, s.rearrange("p j c -> p c j"))
             else:
                 cast(eng, d.rearrange("p (c i) j -> p c j i", i=4), s.rearrange("p j (c i) -> p c j i", i=4))
 
-        def w1cols(eng, g, raw, m0, m1):
-            d = g[:].rearrange("p (t m) j -> p t m j", t=4)[:, :, m0:m1]
-            s = raw[:].rearrange("p j (m t) -> p t m j", t=4)[:, :, m0:m1]
-            if eng == "G":
-                cast(eng, d, s)
-            else:
-                cast(eng, d.rearrange("p t m j -> p m j t"), s.rearrange("p t m j -> p m j t"))
+        def chunk_of(b):
+            pos = 0
+            for ci, ch in enumerate(XCH):
+                if b < pos + ch:
+                    return ci, pos, ch
+                pos += ch
 
-        def psum_op(eng, dst, src, func):
-            if eng == "S":
-                nc.scalar.activation(dst, src, func)
-            elif func == RELU:
-                nc.vector.tensor_scalar(dst, src, 0.0, None, mybir.AluOpType.max)
-            else:
-                nc.vector.tensor_tensor(dst, src, src, MULT)
+        def group_of(groups, e):
+            for g, grp in enumerate(groups):
+                if e in grp:
+                    return g, grp.index(e), len(grp)
 
         for i in TEXT.split(" "):
             if i == "lst":
                 nc.sync.dma_start(lst[:], offs)
             elif i.startswith("x"):
-                a, c = int(i[1]), int(i[2])
-                t = get("x" + i[1:], rxp, [P, 4, 512], F32, "raw")
-                nc.sync.dma_start(t[:], xv[a][:, :, c * 512 : (c + 1) * 512])
+                a, b = int(i[1]), int(i[2])
+                t = get(i, p_raw, [P, 4, 512], F32, "raw")
+                nc.sync.dma_start(t[:], xv[a][:, :, b * 512 : (b + 1) * 512])
             elif i.startswith("w1_"):
                 e, a = int(i[3]), int(i[4])
-                t = get("w1" + i[3:], rwp, [P, 4, 512], F32, "raw")
+                t = get("w1" + i[3:], p_raw, [P, 4, 512], F32, "raw")
                 nc.sync.dma_start(t[:], w1[e].rearrange("(a p j) h -> a p j h", p=P, j=4)[a])
             elif i.startswith("w2_"):
-                t = get("w2" + i[3:], r2p, [P, 4, N], F32, "w2r")
-                nc.sync.dma_start(t[:], w2[int(i[3])].rearrange("(p j) n -> p j n", j=4))
+                g = int(i[3:])
+                grp = CFG["q2"][g]
+                t = get("w2_%d" % g, keep, [P, len(grp), 4, N], F32, "w2r%d" % g)
+                if len(grp) == 1:
+                    nc.sync.dma_start(t[:, 0], w2[grp[0]].rearrange("(p j) n -> p j n", j=4))
+                else:
+                    for k, e in enumerate(grp):
+                        nc.sync.dma_start(t[:, k], w2[e].rearrange("(p j) n -> p j n", j=4))
             elif i == "gate":
                 nc.sync.dma_start(gate_sb[:], gate.rearrange("(b p) j -> p b j", p=P))
             elif i.startswith("ms"):
                 nc.vector.memset(win[int(i[2])][:], 0.0)
             elif i.startswith("cx"):
-                a, c = int(i[3]), int(i[4])
-                g = get("xb" + i[3:], xbp, [P, 512, 4], BF16, "xb")
-                v = CX[3 * a + c]
-                cols(i[2], g, tl["x" + i[3:]], *((0, v) if i[2] == "V" else (v, 512)))
+                a, b = int(i[3]), int(i[4])
+                ci, pos, ch = chunk_of(b)
+                g = get("xb%d%d" % (a, ci), p_xb, [P, 512 * ch, 4], BF16, "xb")
+                v0, v1 = (0, XV) if i[2] == "V" else (XV, 512)
+                o = 512 * (b - pos)
+                cols(i[2], g[:, o + v0 : o + v1, :], tl["x" + i[3:]][:, :, v0:v1])
             elif i.startswith("qx"):
-                a, c = int(i[2]), int(i[3])
-                s = slice(c * 512, (c + 1) * 512)
+                a, ci = int(i[2]), int(i[3])
+                pos, ch = sum(XCH[:ci]), XCH[ci]
+                s = slice(pos * 512, (pos + ch) * 512)
                 nc.vector.quantize_mx(out=xw[a][:, s].bitcast(FP8X4), scales=xs[4 * a : P, s], in_=tl["xb" + i[2:]][:].rearrange("p w j -> p (w j)"))
             elif i.startswith("gw"):
                 a, s = int(i[2]), int(i[3])
@@ -128,32 +129,54 @@ def tile_routed_moe_kernel(tc, xT, w1, w2, gate, offs, out):
                 nc.vector.tensor_copy(xgs[:, j0:j1], xs[:].indirect(lst[:, j0 // 16 : j1 // 16]))
             elif i.startswith("c1"):
                 e, a = int(i[3]), int(i[4])
-                g = get("wb" + i[3:], wbp, [P, 512, 4], BF16, "wb")
-                v, gp = CW1[2 * e + a]
-                w1cols(i[2], g, tl["w1" + i[3:]], *{"V": (0, v), "G": (v, v + gp), "S": (v + gp, 128)}[i[2]])
+                if CFG["qm"][e] == 1:
+                    g = get("wb%d" % e, p_wb, [P, 2, 512, 4], BF16, "wb")[:, a]
+                else:
+                    g = get("wb%d%d" % (e, a), p_wb, [P, 512, 4], BF16, "wb")[:]
+                v, gp = CFG["w1"][e]
+                m0, m1 = {"V": (0, v), "G": (v, v + gp), "S": (v + gp, 128)}[i[2]]
+                d = g.rearrange("p (t m) j -> p t m j", t=4)[:, :, m0:m1]
+                s = tl["w1" + i[3:]][:].rearrange("p j (m t) -> p t m j", t=4)[:, :, m0:m1]
+                if i[2] == "G":
+                    cast("G", d, s)
+                else:
+                    cast(i[2], d.rearrange("p t m j -> p m j t"), s.rearrange("p t m j -> p m j t"))
             elif i.startswith("q1"):
                 e, a = int(i[2]), int(i[3])
                 wc = get("w1c%d" % e, keep, [P, 2, H], U32, "w1c%d" % e)
                 ws = get("w1s%d" % e, keep, [P, 2, H], U8, "w1s%d" % e)
-                nc.vector.quantize_mx(out=wc[:, a, :].bitcast(FP8X4), scales=ws[:, a, :], in_=tl["wb" + i[2:]][:].rearrange("p w j -> p (w j)"))
+                if CFG["qm"][e] == 1:
+                    nc.vector.quantize_mx(
+                        out=wc[:].rearrange("p a h -> p (a h)").bitcast(FP8X4),
+                        scales=ws[:].rearrange("p a h -> p (a h)"),
+                        in_=tl["wb%d" % e][:].rearrange("p a w j -> p (a w j)"),
+                    )
+                else:
+                    nc.vector.quantize_mx(out=wc[:, a, :].bitcast(FP8X4), scales=ws[:, a, :], in_=tl["wb" + i[2:]][:].rearrange("p w j -> p (w j)"))
             elif i.startswith("c2"):
-                e = int(i[3])
-                g = get("w2b" + i[3], hp, [P, N, 4], BF16, "w2b")
-                v, gp = CW2[e]
-                cols(i[2], g, tl["w2" + i[3]], *{"V": (0, v), "G": (v, v + gp), "S": (v + gp, N)}[i[2]])
+                g = int(i[3:])
+                n = len(CFG["q2"][g])
+                wb = get("w2b%d" % g, p_w2b, [P, n, N, 4], BF16, "w2b")
+                f = int(CFG["w2g"] * N)
+                c0, c1 = (0, f) if i[2] == "G" else (f, N)
+                for k in range(n):
+                    cols(i[2], wb[:, k, c0:c1, :], tl["w2_%d" % g][:, k, :, c0:c1])
             elif i.startswith("q2"):
-                e = int(i[2])
-                wc = get("w2c%d" % e, keep, [P, N], U32, "w2c%d" % e)
-                ws = get("w2s%d" % e, keep, [P, N], U8, "w2s%d" % e)
-                nc.vector.quantize_mx(out=wc[:].bitcast(FP8X4), scales=ws[:], in_=tl["w2b" + i[2]][:].rearrange("p w j -> p (w j)"))
+                g = int(i[2:])
+                e0, n = CFG["q2"][g][0], len(CFG["q2"][g])
+                nc.vector.quantize_mx(
+                    out=w2c[:, e0 : e0 + n, :].rearrange("p e n -> p (e n)").bitcast(FP8X4),
+                    scales=w2s[:, e0 : e0 + n, :].rearrange("p e n -> p (e n)"),
+                    in_=tl["w2b%d" % g][:].rearrange("p e w j -> p (e w j)"),
+                )
             elif i.startswith("m1"):
                 e, s = int(i[2]), int(i[3])
-                ph = get("ph" + i[2:], psum_h, [P, 4, 128], F32, "ph")
-                sl = slice(C * e + 128 * s, C * e + 128 * (s + 1))
-                for t in range(4):
+                ph = get("ph" + i[2:], psum_h, [P, 2, C], F32, "ph")
+                sl = slice(C * e, C * (e + 1))
+                for t in (2 * s, 2 * s + 1):
                     for a in range(2):
                         nc.tensor.matmul_mx(
-                            out=ph[:, t, :],
+                            out=ph[:, t - 2 * s, :],
                             lhsT=tl["w1c%d" % e][:, a, P * t : P * (t + 1)].bitcast(FP8X4),
                             lhsT_scale=tl["w1s%d" % e][:, a, P * t : P * (t + 1)],
                             rhs=xg[:, a, sl].bitcast(FP8X4),
@@ -162,22 +185,26 @@ def tile_routed_moe_kernel(tc, xT, w1, w2, gate, offs, out):
                             stop=(a == 1),
                         )
             elif i.startswith("r"):
-                r = get("r" + i[1:], hp, [P, 128, 4], F32, "r")
-                psum_op(RL[2 * int(i[1]) + int(i[2])], r[:], tl["ph" + i[1:]][:].rearrange("p t n -> p n t"), RELU)
+                e, s = int(i[1]), int(i[2])
+                r = get("r%d" % e, p_r, [P, 2, C, 2], F32, "r")[:, s]
+                src = tl["ph" + i[1:]][:].rearrange("p t n -> p n t")
+                if CFG["rl"][e] == "S":
+                    nc.scalar.activation(r, src, RELU)
+                else:
+                    nc.vector.tensor_scalar(r, src, 0.0, None, mybir.AluOpType.max)
             elif i.startswith("qh"):
                 e = int(i[2])
-                hc = get("hc%d" % e, hp, [P, C], U32, "hc")
-                hs = get("hs%d" % e, hp, [P, C], U8, "hs")
-                s0, s1 = (0, C) if not HQ else (128 * int(i[3]), 128 * int(i[3]) + 128)
-                nc.vector.quantize_mx(out=hc[:, s0:s1].bitcast(FP8X4), scales=hs[:, s0:s1], in_=tl["hb%d" % e][:, s0:s1, :].rearrange("p w j -> p (w j)"))
+                hc = get("hc%d" % e, p_hc, [P, C], U32, "hc")
+                hs = get("hs%d" % e, p_hc, [P, C], U8, "hs")
+                nc.vector.quantize_mx(out=hc[:].bitcast(FP8X4), scales=hs[:], in_=tl["hb%d" % e][:].rearrange("p w j -> p (w j)"))
             elif i.startswith("m2"):
                 e = int(i[2])
                 y = get("y%d" % e, psum_y, [P, 2, C], F32, "y")
                 for b in range(2):
                     nc.tensor.matmul_mx(
                         out=y[:, b, :],
-                        lhsT=tl["w2c%d" % e][:, P * b : P * (b + 1)].bitcast(FP8X4),
-                        lhsT_scale=tl["w2s%d" % e][:, P * b : P * (b + 1)],
+                        lhsT=w2c[:, e, P * b : P * (b + 1)].bitcast(FP8X4),
+                        lhsT_scale=w2s[:, e, P * b : P * (b + 1)],
                         rhs=tl["hc%d" % e][:].bitcast(FP8X4),
                         rhs_scale=tl["hs%d" % e][:],
                         start=True,
@@ -185,22 +212,30 @@ def tile_routed_moe_kernel(tc, xT, w1, w2, gate, offs, out):
                     )
             elif i.startswith("y"):
                 e = int(i[1])
-                ys = get("ys%d" % e, hp, [P, 2, C], F32, "ys")
-                if EV[e] == "S":
-                    nc.scalar.copy(ys[:], tl["y%d" % e][:])
+                g, k, n = group_of(CFG["scg"], e)
+                ys = get("ys%d" % g, p_ys, [P, 2, n * C], F32, "ys")[:, :, k * C : (k + 1) * C]
+                if CFG["ev"] == "S":
+                    nc.scalar.copy(ys, tl["y%d" % e][:])
                 else:
-                    nc.vector.tensor_tensor(ys[:], tl["y%d" % e][:], gate_sb[:, :, C * e : C * (e + 1)], MULT)
+                    nc.vector.tensor_tensor(ys, tl["y%d" % e][:], gate_sb[:, :, C * e : C * (e + 1)], MULT)
             elif i.startswith("sc"):
-                e, b = int(i[2]), int(i[3])
-                w = win[b][:].indirect(lst[:, 16 * e : 16 * (e + 1)])
-                if EV[e] == "S":
-                    nc.vector.tensor_tensor(w, tl["ys%d" % e][:, b, :], gate_sb[:, b, C * e : C * (e + 1)], MULT)
+                g, b = int(i[2]), int(i[3])
+                e0, n = CFG["scg"][g][0], len(CFG["scg"][g])
+                w = win[b][:].indirect(lst[:, 16 * e0 : 16 * (e0 + n)])
+                if CFG["ev"] == "S":
+                    nc.vector.tensor_tensor(w, tl["ys%d" % g][:, b, :], gate_sb[:, b, C * e0 : C * (e0 + n)], MULT)
                 else:
-                    nc.vector.tensor_copy(w, tl["ys%d" % e][:, b, :])
+                    nc.vector.tensor_copy(w, tl["ys%d" % g][:, b, :])
             elif i.startswith("st"):
                 b = int(i[2])
                 nc.sync.dma_start(out[P * b : P * (b + 1), :], win[b][:])
             elif i.startswith("s"):
                 e, s = int(i[1]), int(i[2])
-                hb = get("hb%d" % e, hbp, [P, C, 4], BF16, "hb")
-                psum_op(SQ[2 * e + s], hb[:, 128 * s : 128 * (s + 1), :], tl["r" + i[1:]][:], SQUARE)
+                hb = get("hb%d" % e, p_hb, [P, C, 4], BF16, "hb")
+                sl = slice(0, C) if CFG["sqm"][e] == 1 else slice(128 * s, 128 * (s + 1))
+                r = tl["r%d" % e][:, :, sl, :].rearrange("p u n t -> p n u t")
+                d = hb[:, sl, :].rearrange("p n (u t) -> p n u t", u=2)
+                if (CFG["sqe"][e] == "S") != (s == 1):
+                    nc.scalar.activation(d, r, SQUARE)
+                else:
+                    nc.vector.tensor_tensor(d, r, r, MULT)

@@ -15,8 +15,8 @@ ADD = mybir.AluOpType.add
 RELU = mybir.ActivationFunctionType.Relu
 SQUARE = mybir.ActivationFunctionType.Square
 P = 128
-CFG = {"xch":[1,1,1],"xv":192,"q2":[[0,1],[2,3]],"w2g":0.5,"gs":[[4],[4],[4]],"qm":[1,2,2,2],"w1":[[0,0],[0,64],[0,64],[48,32]],"rl":["V","S","S","S"],"sqm":[2,1,1,2],"sqe":["V","S","S","S"],"ev":"S","scg":[[0],[1],[2],[3]],"ld":"D","ord":1}
-TEXT = """lst x00 x01 x02 x10 x11 x12 w1_00 w1_01 w2_0 w1_10 w1_11 gate w1_20 w1_21 w1_30 w1_31 w2_1 ms0 ms1 cxV00 cxS00 qx00 cxV01 cxS01 qx01 cxV02 cxS02 qx02 gw00 cxV10 cxS10 qx10 cxV11 cxS11 qx11 cxV12 cxS12 qx12 c1S00 c1S01 q100 gw10 gb0 m100 r00 m101 r01 s00 s01 qh0 c2G0 c2S0 q20 m20 y0 c1G10 c1S10 c1G11 c1S11 q110 q111 sc00 sc01 m110 r10 m111 r11 s10 qh1 m21 y1 c1G20 c1S20 c1G21 c1S21 q120 q121 sc10 sc11 m120 r20 m121 r21 s20 qh2 c2G1 c2S1 q21 m22 y2 c1V30 c1G30 c1S30 c1V31 c1G31 c1S31 q130 q131 sc20 sc21 m130 r30 m131 r31 s30 s31 qh3 m23 y3 sc30 sc31 st0 st1"""
+CFG = {"xch":[1,1,1],"xv":160,"q2":[[0],[1],[2,3]],"w2g":0,"gs":[[4],[4],[4]],"qm":[1,1,1,1],"w1":[[0,0],[64,0],[64,0],[64,0]],"rl":["S","S","S","S"],"sqm":[2,1,1,2],"sqe":["S","S","S","S"],"ev":"S","scg":[[0],[1],[2],[3]],"ld":"D","ord":2}
+TEXT = """lst x00 x01 x02 x10 x11 x12 w1_00 w1_01 w2_0 w1_10 w1_11 gate w2_1 w1_20 w1_21 w1_30 w1_31 w2_2 ms0 ms1 cxV00 cxS00 qx00 cxV01 cxS01 qx01 cxV02 cxS02 qx02 gw00 cxV10 cxS10 qx10 cxV11 cxS11 qx11 cxV12 cxS12 qx12 c1S00 c1S01 q100 gw10 gb0 m100 r00 m101 r01 s00 s01 qh0 c2S0 q20 m20 y0 sc00 sc01 c1V10 c1S10 c1V11 c1S11 q110 m110 r10 m111 r11 s10 qh1 c2S1 q21 m21 y1 sc10 sc11 c1V20 c1S20 c1V21 c1S21 q120 m120 r20 m121 r21 s20 qh2 c2S2 q22 m22 y2 sc20 sc21 c1V30 c1S30 c1V31 c1S31 q130 m130 r30 m131 r31 s30 s31 qh3 m23 y3 sc30 sc31 st0 st1"""
 
 
 def tile_routed_moe_kernel(tc, xT, w1, w2, gate, offs, out):

@@ -15,8 +15,8 @@ ADD = mybir.AluOpType.add
 RELU = mybir.ActivationFunctionType.Relu
 SQUARE = mybir.ActivationFunctionType.Square
 P = 128
-CFG = {"xch":[1,1,1],"xv":160,"q2":[[0],[1],[2,3]],"w2g":0,"gs":[[4],[4],[4]],"qm":[1,1,1,1],"w1":[[0,0],[64,0],[64,0],[64,0]],"rl":["S","S","S","S"],"sqm":[2,1,1,2],"sqe":["S","S","S","S"],"ev":"S","scg":[[0],[1],[2],[3]],"ld":"D","ord":2}
-TEXT = """lst x00 x01 x02 x10 x11 x12 w1_00 w1_01 w2_0 w1_10 w1_11 gate w2_1 w1_20 w1_21 w1_30 w1_31 w2_2 ms0 ms1 cxV00 cxS00 qx00 cxV01 cxS01 qx01 cxV02 cxS02 qx02 gw00 cxV10 cxS10 qx10 cxV11 cxS11 qx11 cxV12 cxS12 qx12 c1S00 c1S01 q100 gw10 gb0 m100 r00 m101 r01 s00 s01 qh0 c2S0 q20 m20 y0 sc00 sc01 c1V10 c1S10 c1V11 c1S11 q110 m110 r10 m111 r11 s10 qh1 c2S1 q21 m21 y1 sc10 sc11 c1V20 c1S20 c1V21 c1S21 q120 m120 r20 m121 r21 s20 qh2 c2S2 q22 m22 y2 sc20 sc21 c1V30 c1S30 c1V31 c1S31 q130 m130 r30 m131 r31 s30 s31 qh3 m23 y3 sc30 sc31 st0 st1"""
+CFG = {"xch":[1,1,1],"xv":192,"q2":[[0],[1],[2],[3]],"w2g":1,"gs":[[4],[1,3],[1,3]],"qm":[1,2,2,2],"w1":[[0,48],[0,64],[0,48],[48,32]],"rl":["S","S","S","S"],"sqm":[1,1,1,1],"sqe":["S","S","S","S"],"ev":"V","scg":[[0],[1],[2],[3]],"ld":"E","ord":0}
+TEXT = """lst x00 x01 x02 w1_00 w1_01 x10 x11 x12 w2_0 w1_10 w1_11 gate w2_1 w1_20 w1_21 w2_2 w1_30 w1_31 w2_3 ms0 ms1 cxV00 cxS00 qx00 cxV01 cxS01 qx01 cxV02 cxS02 qx02 gw00 cxV10 cxS10 qx10 cxV11 cxS11 qx11 cxV12 cxS12 qx12 c1G00 c1S00 c1G01 c1S01 q100 gw10 gb0 m100 r00 m101 r01 s00 qh0 c2G0 q20 m20 y0 c1G10 c1S10 c1G11 c1S11 q110 gw11 gb1 q111 m110 r10 m111 r11 s10 qh1 c2G1 q21 m21 y1 sc00 sc01 c1G20 c1S20 c1G21 c1S21 q120 q121 m120 r20 m121 r21 s20 qh2 c2G2 q22 m22 y2 sc10 sc11 c1V30 c1G30 c1S30 c1V31 c1G31 c1S31 q130 q131 m130 r30 m131 r31 s30 qh3 c2G3 q23 m23 y3 sc20 sc21 sc30 sc31 st0 st1"""
 
 
 def tile_routed_moe_kernel(tc, xT, w1, w2, gate, offs, out):

@@ -4,6 +4,7 @@ import concourse.mybir as mybir
 
 K, T, E, C, H, N = 1024, 1536, 4, 256, 512, 256
 FLOPS = 2 * E * C * (K * H + H * N)
+
 F32 = mybir.dt.float32
 BF16 = mybir.dt.bfloat16
 U32 = mybir.dt.uint32
@@ -11,231 +12,223 @@ U16 = mybir.dt.uint16
 U8 = mybir.dt.uint8
 FP8X4 = mybir.dt.float8_e4m3fn_x4
 MULT = mybir.AluOpType.mult
-ADD = mybir.AluOpType.add
 RELU = mybir.ActivationFunctionType.Relu
 SQUARE = mybir.ActivationFunctionType.Square
+
 P = 128
-CFG = {"xch":[1,1,1],"xv":192,"q2":[[0],[1],[2],[3]],"w2g":1,"gs":[[4],[1,3],[1,3]],"qm":[1,2,2,2],"w1":[[0,48],[0,64],[0,48],[48,32]],"rl":["S","S","S","S"],"sqm":[1,1,1,1],"sqe":["S","S","S","S"],"ev":"V","scg":[[0],[1],[2],[3]],"ld":"E","ord":0}
-TEXT = """lst x00 x01 x02 w1_00 w1_01 x10 x11 x12 w2_0 w1_10 w1_11 gate w2_1 w1_20 w1_21 w2_2 w1_30 w1_31 w2_3 ms0 ms1 cxV00 cxS00 qx00 cxV01 cxS01 qx01 cxV02 cxS02 qx02 gw00 cxV10 cxS10 qx10 cxV11 cxS11 qx11 cxV12 cxS12 qx12 c1G00 c1S00 c1G01 c1S01 q100 gw10 gb0 m100 r00 m101 r01 s00 qh0 c2G0 q20 m20 y0 c1G10 c1S10 c1G11 c1S11 q110 gw11 gb1 q111 m110 r10 m111 r11 s10 qh1 c2G1 q21 m21 y1 sc00 sc01 c1G20 c1S20 c1G21 c1S21 q120 q121 m120 r20 m121 r21 s20 qh2 c2G2 q22 m22 y2 sc10 sc11 c1V30 c1G30 c1S30 c1V31 c1G31 c1S31 q130 q131 m130 r30 m131 r31 s30 qh3 c2G3 q23 m23 y3 sc20 sc21 sc30 sc31 st0 st1"""
+PACK = 4
+PASSES = K // (P * PACK)
+TILES = H // P
+BANK_TILES = 2
+OUT_TILES = N // P
+LIST_ROWS = 16
+CHUNK = 512
+
+X_VECTOR = 192
+W1_VECTOR = (0, 64, 32, 48)
+
+
+def interleave(copy, grouped, raw):
+    copy(
+        grouped.rearrange("p (c i) j -> p c j i", i=4),
+        raw.rearrange("p j (c i) -> p c j i", i=4),
+    )
+
+
+def interleave_w1(copy, grouped, raw, first, last):
+    copy(
+        grouped.rearrange("p (t m) j -> p m j t", t=TILES)[:, first:last],
+        raw.rearrange("p j (m t) -> p m j t", t=TILES)[:, first:last],
+    )
 
 
 def tile_routed_moe_kernel(tc, xT, w1, w2, gate, offs, out):
     nc = tc.nc
     with ExitStack() as ctx:
         keep = ctx.enter_context(tc.tile_pool(name="keep", bufs=1))
-        p_raw = ctx.enter_context(tc.tile_pool(name="p_raw", bufs=11))
-        p_xb = ctx.enter_context(tc.tile_pool(name="p_xb", bufs=2))
-        p_wb = ctx.enter_context(tc.tile_pool(name="p_wb", bufs=2))
-        p_w2b = ctx.enter_context(tc.tile_pool(name="p_w2b", bufs=2))
-        p_r = ctx.enter_context(tc.tile_pool(name="p_r", bufs=2))
-        p_hb = ctx.enter_context(tc.tile_pool(name="p_hb", bufs=2))
-        p_hc = ctx.enter_context(tc.tile_pool(name="p_hc", bufs=3))
-        p_ys = ctx.enter_context(tc.tile_pool(name="p_ys", bufs=2))
-        psum_h = ctx.enter_context(tc.psum_pool(name="psum_h", bufs=4))
-        psum_y = ctx.enter_context(tc.psum_pool(name="psum_y", bufs=3))
-        xv = xT.rearrange("(a p j) n -> a p j n", p=P, j=4)
-        tl = {}
-        lst = keep.tile([P, E * C // 16], U16, name="lst")
-        xw = [keep.tile([P, T], U32, name=f"xw{a}", align_bytes=64) for a in range(2)]
-        xs = keep.tile([P, T], U8, name="xs", align_bytes=64)
-        nc.gpsimd.memset(xs[:], 0)
-        win = [keep.tile([P, T], F32, name=f"win{b}", align_bytes=64) for b in range(2)]
-        xg = keep.tile([P, 2, E * C], U32, name="xg", align_bytes=64)
-        xgs = keep.tile([P, E * C], U8, name="xgs", align_bytes=64)
-        gate_sb = keep.tile([P, 2, E * C], F32, name="gate_sb")
-        XCH, XV, GS = CFG["xch"], CFG["xv"], CFG["gs"]
-        w2c = keep.tile([P, E, N], U32, name="w2c", align_bytes=64)
-        w2s = keep.tile([P, E, N], U8, name="w2s", align_bytes=64)
+        raw_pool = ctx.enter_context(tc.tile_pool(name="raw_pool", bufs=11))
+        x_pool = ctx.enter_context(tc.tile_pool(name="x_pool", bufs=2))
+        w1_pool = ctx.enter_context(tc.tile_pool(name="w1_pool", bufs=2))
+        w2_pool = ctx.enter_context(tc.tile_pool(name="w2_pool", bufs=2))
+        relu_pool = ctx.enter_context(tc.tile_pool(name="relu_pool", bufs=2))
+        h_pool = ctx.enter_context(tc.tile_pool(name="h_pool", bufs=2))
+        h_codes_pool = ctx.enter_context(tc.tile_pool(name="h_codes_pool", bufs=3))
+        y_pool = ctx.enter_context(tc.tile_pool(name="y_pool", bufs=2))
+        h_psum = ctx.enter_context(tc.psum_pool(name="h_psum", bufs=5))
+        y_psum = ctx.enter_context(tc.psum_pool(name="y_psum", bufs=3))
 
-        def get(key, pool, shape, dt, tag):
-            if key not in tl:
-                if pool is psum_h or pool is psum_y:
-                    tl[key] = pool.tile(shape, dt, name=tag)
-                else:
-                    tl[key] = pool.tile(shape, dt, name=tag, align_bytes=64)
-            return tl[key]
+        slots_list = keep.tile([P, E * C // LIST_ROWS], U16, name="slots_list", align_bytes=64)
+        words = [keep.tile([P, T], U32, name=f"words{a}", align_bytes=64) for a in range(PASSES)]
+        scales = keep.tile([P, T], U8, name="scales", align_bytes=64)
+        nc.gpsimd.memset(scales[:], 0)
+        windows = [keep.tile([P, T], F32, name=f"window{b}", align_bytes=64) for b in range(OUT_TILES)]
+        slot_words = keep.tile([P, PASSES, E * C], U32, name="slot_words", align_bytes=64)
+        slot_scales = keep.tile([P, E * C], U8, name="slot_scales", align_bytes=64)
+        gate_sb = keep.tile([P, OUT_TILES, E * C], F32, name="gate_sb", align_bytes=64)
+        w2_words = keep.tile([P, E, N], U32, name="w2_words", align_bytes=64)
+        w2_scales = keep.tile([P, E, N], U8, name="w2_scales", align_bytes=64)
 
-        def cast(eng, dst, src):
-            if eng == "V":
-                nc.vector.tensor_copy(dst, src)
-            elif eng == "S":
-                nc.scalar.copy(dst, src)
-            else:
-                nc.gpsimd.tensor_scalar(dst, src, 1.0, 0.0, MULT, ADD)
+        x_raw, w1_raw, w2_raw, w1_words, w1_scales = {}, {}, {}, {}, {}
 
-        def cols(eng, d, s):
-            if eng == "G":
-                cast(eng, d, s.rearrange("p j c -> p c j"))
-            else:
-                cast(eng, d.rearrange("p (c i) j -> p c j i", i=4), s.rearrange("p j (c i) -> p c j i", i=4))
+        def load_x(a):
+            rows = xT.rearrange("(a p j) n -> a p j n", p=P, j=PACK)[a]
+            for c in range(T // CHUNK):
+                x_raw[a, c] = raw_pool.tile([P, PACK, CHUNK], F32, name="raw", align_bytes=64)
+                nc.sync.dma_start(x_raw[a, c][:], rows[:, :, c * CHUNK : (c + 1) * CHUNK])
 
-        def chunk_of(b):
-            pos = 0
-            for ci, ch in enumerate(XCH):
-                if b < pos + ch:
-                    return ci, pos, ch
-                pos += ch
+        def load_w1(e):
+            for a in range(PASSES):
+                w1_raw[e, a] = raw_pool.tile([P, PACK, H], F32, name="raw", align_bytes=64)
+                nc.sync.dma_start(w1_raw[e, a][:], w1[e].rearrange("(a p j) h -> a p j h", p=P, j=PACK)[a])
 
-        def group_of(groups, e):
-            for g, grp in enumerate(groups):
-                if e in grp:
-                    return g, grp.index(e), len(grp)
+        def load_w2(pair):
+            w2_raw[pair] = keep.tile([P, 2, PACK, N], F32, name=f"w2_raw{pair}", align_bytes=64)
+            for i in range(2):
+                nc.sync.dma_start(w2_raw[pair][:, i], w2[2 * pair + i].rearrange("(p j) n -> p j n", j=PACK))
 
-        for i in TEXT.split(" "):
-            if i == "lst":
-                nc.sync.dma_start(lst[:], offs)
-            elif i.startswith("x"):
-                a, b = int(i[1]), int(i[2])
-                t = get(i, p_raw, [P, 4, 512], F32, "raw")
-                nc.sync.dma_start(t[:], xv[a][:, :, b * 512 : (b + 1) * 512])
-            elif i.startswith("w1_"):
-                e, a = int(i[3]), int(i[4])
-                t = get("w1" + i[3:], p_raw, [P, 4, 512], F32, "raw")
-                nc.sync.dma_start(t[:], w1[e].rearrange("(a p j) h -> a p j h", p=P, j=4)[a])
-            elif i.startswith("w2_"):
-                g = int(i[3:])
-                grp = CFG["q2"][g]
-                t = get("w2_%d" % g, keep, [P, len(grp), 4, N], F32, "w2r%d" % g)
-                if len(grp) == 1:
-                    nc.sync.dma_start(t[:, 0], w2[grp[0]].rearrange("(p j) n -> p j n", j=4))
-                else:
-                    for k, e in enumerate(grp):
-                        nc.sync.dma_start(t[:, k], w2[e].rearrange("(p j) n -> p j n", j=4))
-            elif i == "gate":
-                nc.sync.dma_start(gate_sb[:], gate.rearrange("(b p) j -> p b j", p=P))
-            elif i.startswith("ms"):
-                nc.vector.memset(win[int(i[2])][:], 0.0)
-            elif i.startswith("cx"):
-                a, b = int(i[3]), int(i[4])
-                ci, pos, ch = chunk_of(b)
-                g = get("xb%d%d" % (a, ci), p_xb, [P, 512 * ch, 4], BF16, "xb")
-                v0, v1 = (0, XV) if i[2] == "V" else (XV, 512)
-                o = 512 * (b - pos)
-                cols(i[2], g[:, o + v0 : o + v1, :], tl["x" + i[3:]][:, :, v0:v1])
-            elif i.startswith("qx"):
-                a, ci = int(i[2]), int(i[3])
-                pos, ch = sum(XCH[:ci]), XCH[ci]
-                s = slice(pos * 512, (pos + ch) * 512)
-                nc.vector.quantize_mx(out=xw[a][:, s].bitcast(FP8X4), scales=xs[4 * a : P, s], in_=tl["xb" + i[2:]][:].rearrange("p w j -> p (w j)"))
-            elif i.startswith("gw"):
-                a, s = int(i[2]), int(i[3])
-                j0 = 256 * sum(GS[a][:s])
-                j1 = j0 + 256 * GS[a][s]
-                nc.vector.tensor_copy(xg[:, a, j0:j1], xw[a][:].indirect(lst[:, j0 // 16 : j1 // 16]))
-            elif i.startswith("gb"):
-                s = int(i[2])
-                j0 = 256 * sum(GS[2][:s])
-                j1 = j0 + 256 * GS[2][s]
-                nc.vector.tensor_copy(xgs[:, j0:j1], xs[:].indirect(lst[:, j0 // 16 : j1 // 16]))
-            elif i.startswith("c1"):
-                e, a = int(i[3]), int(i[4])
-                if CFG["qm"][e] == 1:
-                    g = get("wb%d" % e, p_wb, [P, 2, 512, 4], BF16, "wb")[:, a]
-                else:
-                    g = get("wb%d%d" % (e, a), p_wb, [P, 512, 4], BF16, "wb")[:]
-                v, gp = CFG["w1"][e]
-                m0, m1 = {"V": (0, v), "G": (v, v + gp), "S": (v + gp, 128)}[i[2]]
-                d = g.rearrange("p (t m) j -> p t m j", t=4)[:, :, m0:m1]
-                s = tl["w1" + i[3:]][:].rearrange("p j (m t) -> p t m j", t=4)[:, :, m0:m1]
-                if i[2] == "G":
-                    cast("G", d, s)
-                else:
-                    cast(i[2], d.rearrange("p t m j -> p m j t"), s.rearrange("p t m j -> p m j t"))
-            elif i.startswith("q1"):
-                e, a = int(i[2]), int(i[3])
-                wc = get("w1c%d" % e, keep, [P, 2, H], U32, "w1c%d" % e)
-                ws = get("w1s%d" % e, keep, [P, 2, H], U8, "w1s%d" % e)
-                if CFG["qm"][e] == 1:
-                    nc.vector.quantize_mx(
-                        out=wc[:].rearrange("p a h -> p (a h)").bitcast(FP8X4),
-                        scales=ws[:].rearrange("p a h -> p (a h)"),
-                        in_=tl["wb%d" % e][:].rearrange("p a w j -> p (a w j)"),
-                    )
-                else:
-                    nc.vector.quantize_mx(out=wc[:, a, :].bitcast(FP8X4), scales=ws[:, a, :], in_=tl["wb" + i[2:]][:].rearrange("p w j -> p (w j)"))
-            elif i.startswith("c2"):
-                g = int(i[3:])
-                n = len(CFG["q2"][g])
-                wb = get("w2b%d" % g, p_w2b, [P, n, N, 4], BF16, "w2b")
-                f = int(CFG["w2g"] * N)
-                c0, c1 = (0, f) if i[2] == "G" else (f, N)
-                for k in range(n):
-                    cols(i[2], wb[:, k, c0:c1, :], tl["w2_%d" % g][:, k, :, c0:c1])
-            elif i.startswith("q2"):
-                g = int(i[2:])
-                e0, n = CFG["q2"][g][0], len(CFG["q2"][g])
+        nc.sync.dma_start(slots_list[:], offs)
+        load_x(0)
+        load_x(1)
+        load_w1(0)
+        load_w2(0)
+        load_w1(1)
+        load_w1(2)
+        nc.sync.dma_start(gate_sb[:], gate.rearrange("(b p) j -> p b j", p=P))
+        load_w1(3)
+        load_w2(1)
+
+        for b in range(OUT_TILES):
+            nc.vector.memset(windows[b][:], 0.0)
+
+        def quantise_x(a):
+            for c in range(T // CHUNK):
+                grouped = x_pool.tile([P, CHUNK, PACK], BF16, name="x_grouped", align_bytes=64)
+                raw = x_raw[a, c]
+                interleave(nc.vector.tensor_copy, grouped[:, :X_VECTOR], raw[:, :, :X_VECTOR])
+                interleave(nc.scalar.copy, grouped[:, X_VECTOR:], raw[:, :, X_VECTOR:])
+                tokens = slice(c * CHUNK, (c + 1) * CHUNK)
                 nc.vector.quantize_mx(
-                    out=w2c[:, e0 : e0 + n, :].rearrange("p e n -> p (e n)").bitcast(FP8X4),
-                    scales=w2s[:, e0 : e0 + n, :].rearrange("p e n -> p (e n)"),
-                    in_=tl["w2b%d" % g][:].rearrange("p e w j -> p (e w j)"),
+                    out=words[a][:, tokens].bitcast(FP8X4),
+                    scales=scales[4 * a : P, tokens],
+                    in_=grouped[:].rearrange("p c j -> p (c j)"),
                 )
-            elif i.startswith("m1"):
-                e, s = int(i[2]), int(i[3])
-                ph = get("ph" + i[2:], psum_h, [P, 2, C], F32, "ph")
-                sl = slice(C * e, C * (e + 1))
-                for t in (2 * s, 2 * s + 1):
-                    for a in range(2):
+
+        def gather_words(a):
+            nc.vector.tensor_copy(slot_words[:, a, :], words[a][:].indirect(slots_list[:]))
+
+        def gather_scales():
+            nc.vector.tensor_copy(slot_scales[:], scales[:].indirect(slots_list[:]))
+
+        def quantise_w1(e):
+            w1_words[e] = keep.tile([P, PASSES, H], U32, name=f"w1_words{e}", align_bytes=64)
+            w1_scales[e] = keep.tile([P, PASSES, H], U8, name=f"w1_scales{e}", align_bytes=64)
+            at_once = PASSES if e == 0 else 1
+            vector = W1_VECTOR[e]
+            for a0 in range(0, PASSES, at_once):
+                grouped = w1_pool.tile([P, at_once, H, PACK], BF16, name="w1_grouped", align_bytes=64)
+                for i in range(at_once):
+                    raw = w1_raw[e, a0 + i][:]
+                    if vector > 0:
+                        interleave_w1(nc.vector.tensor_copy, grouped[:, i], raw, 0, vector)
+                    interleave_w1(nc.scalar.copy, grouped[:, i], raw, vector, P)
+                nc.vector.quantize_mx(
+                    out=w1_words[e][:, a0 : a0 + at_once].rearrange("p a h -> p (a h)").bitcast(FP8X4),
+                    scales=w1_scales[e][:, a0 : a0 + at_once].rearrange("p a h -> p (a h)"),
+                    in_=grouped[:].rearrange("p a h j -> p (a h j)"),
+                )
+
+        def quantise_w2(pair):
+            grouped = w2_pool.tile([P, 2, N, PACK], BF16, name="w2_grouped", align_bytes=64)
+            for i in range(2):
+                interleave(nc.scalar.copy, grouped[:, i], w2_raw[pair][:, i])
+            experts = slice(2 * pair, 2 * pair + 2)
+            nc.vector.quantize_mx(
+                out=w2_words[:, experts].rearrange("p e n -> p (e n)").bitcast(FP8X4),
+                scales=w2_scales[:, experts].rearrange("p e n -> p (e n)"),
+                in_=grouped[:].rearrange("p e n j -> p (e n j)"),
+            )
+
+        def layer1(e):
+            slots = slice(C * e, C * (e + 1))
+            relu = relu_pool.tile([P, TILES // BANK_TILES, C, BANK_TILES], F32, name="relu", align_bytes=64)
+            for u in range(TILES // BANK_TILES):
+                sums = h_psum.tile([P, BANK_TILES, C], F32, name="h_sums")
+                for i in range(BANK_TILES):
+                    t = BANK_TILES * u + i
+                    columns = slice(P * t, P * (t + 1))
+                    for a in range(PASSES):
                         nc.tensor.matmul_mx(
-                            out=ph[:, t - 2 * s, :],
-                            lhsT=tl["w1c%d" % e][:, a, P * t : P * (t + 1)].bitcast(FP8X4),
-                            lhsT_scale=tl["w1s%d" % e][:, a, P * t : P * (t + 1)],
-                            rhs=xg[:, a, sl].bitcast(FP8X4),
-                            rhs_scale=xgs[4 * a : P, sl],
+                            out=sums[:, i],
+                            lhsT=w1_words[e][:, a, columns].bitcast(FP8X4),
+                            lhsT_scale=w1_scales[e][:, a, columns],
+                            rhs=slot_words[:, a, slots].bitcast(FP8X4),
+                            rhs_scale=slot_scales[4 * a : P, slots],
                             start=(a == 0),
-                            stop=(a == 1),
+                            stop=(a == PASSES - 1),
                         )
-            elif i.startswith("r"):
-                e, s = int(i[1]), int(i[2])
-                r = get("r%d" % e, p_r, [P, 2, C, 2], F32, "r")[:, s]
-                src = tl["ph" + i[1:]][:].rearrange("p t n -> p n t")
-                if CFG["rl"][e] == "S":
-                    nc.scalar.activation(r, src, RELU)
-                else:
-                    nc.vector.tensor_scalar(r, src, 0.0, None, mybir.AluOpType.max)
-            elif i.startswith("qh"):
-                e = int(i[2])
-                hc = get("hc%d" % e, p_hc, [P, C], U32, "hc")
-                hs = get("hs%d" % e, p_hc, [P, C], U8, "hs")
-                nc.vector.quantize_mx(out=hc[:].bitcast(FP8X4), scales=hs[:], in_=tl["hb%d" % e][:].rearrange("p w j -> p (w j)"))
-            elif i.startswith("m2"):
-                e = int(i[2])
-                y = get("y%d" % e, psum_y, [P, 2, C], F32, "y")
-                for b in range(2):
-                    nc.tensor.matmul_mx(
-                        out=y[:, b, :],
-                        lhsT=w2c[:, e, P * b : P * (b + 1)].bitcast(FP8X4),
-                        lhsT_scale=w2s[:, e, P * b : P * (b + 1)],
-                        rhs=tl["hc%d" % e][:].bitcast(FP8X4),
-                        rhs_scale=tl["hs%d" % e][:],
-                        start=True,
-                        stop=True,
-                    )
-            elif i.startswith("y"):
-                e = int(i[1])
-                g, k, n = group_of(CFG["scg"], e)
-                ys = get("ys%d" % g, p_ys, [P, 2, n * C], F32, "ys")[:, :, k * C : (k + 1) * C]
-                if CFG["ev"] == "S":
-                    nc.scalar.copy(ys, tl["y%d" % e][:])
-                else:
-                    nc.vector.tensor_tensor(ys, tl["y%d" % e][:], gate_sb[:, :, C * e : C * (e + 1)], MULT)
-            elif i.startswith("sc"):
-                g, b = int(i[2]), int(i[3])
-                e0, n = CFG["scg"][g][0], len(CFG["scg"][g])
-                w = win[b][:].indirect(lst[:, 16 * e0 : 16 * (e0 + n)])
-                if CFG["ev"] == "S":
-                    nc.vector.tensor_tensor(w, tl["ys%d" % g][:, b, :], gate_sb[:, b, C * e0 : C * (e0 + n)], MULT)
-                else:
-                    nc.vector.tensor_copy(w, tl["ys%d" % g][:, b, :])
-            elif i.startswith("st"):
-                b = int(i[2])
-                nc.sync.dma_start(out[P * b : P * (b + 1), :], win[b][:])
-            elif i.startswith("s"):
-                e, s = int(i[1]), int(i[2])
-                hb = get("hb%d" % e, p_hb, [P, C, 4], BF16, "hb")
-                sl = slice(0, C) if CFG["sqm"][e] == 1 else slice(128 * s, 128 * (s + 1))
-                r = tl["r%d" % e][:, :, sl, :].rearrange("p u n t -> p n u t")
-                d = hb[:, sl, :].rearrange("p n (u t) -> p n u t", u=2)
-                if (CFG["sqe"][e] == "S") != (s == 1):
-                    nc.scalar.activation(d, r, SQUARE)
-                else:
-                    nc.vector.tensor_tensor(d, r, r, MULT)
+                nc.scalar.activation(relu[:, u], sums[:].rearrange("p i n -> p n i"), RELU)
+
+            grouped = h_pool.tile([P, C, PACK], BF16, name="h_grouped", align_bytes=64)
+
+            def views(first, last):
+                return (
+                    grouped[:, first:last].rearrange("p n (u i) -> p n u i", u=TILES // BANK_TILES),
+                    relu[:, :, first:last].rearrange("p u n i -> p n u i"),
+                )
+
+            scalar_slots = C // 2 if e in (0, E - 1) else C
+            squared, source = views(0, scalar_slots)
+            nc.scalar.activation(squared, source, SQUARE)
+            if scalar_slots < C:
+                squared, source = views(scalar_slots, C)
+                nc.vector.tensor_tensor(squared, source, source, MULT)
+
+            h_words = h_codes_pool.tile([P, C], U32, name="h_words", align_bytes=64)
+            h_scales = h_codes_pool.tile([P, C], U8, name="h_scales", align_bytes=64)
+            nc.vector.quantize_mx(
+                out=h_words[:].bitcast(FP8X4), scales=h_scales[:], in_=grouped[:].rearrange("p n j -> p (n j)")
+            )
+            return h_words, h_scales
+
+        def layer2(e, h_words, h_scales):
+            y = y_pool.tile([P, OUT_TILES, C], F32, name="y", align_bytes=64)
+            for b in range(OUT_TILES):
+                features = slice(P * b, P * (b + 1))
+                sums = y_psum.tile([P, C], F32, name="y_sums")
+                nc.tensor.matmul_mx(
+                    out=sums[:],
+                    lhsT=w2_words[:, e, features].bitcast(FP8X4),
+                    lhsT_scale=w2_scales[:, e, features],
+                    rhs=h_words[:].bitcast(FP8X4),
+                    rhs_scale=h_scales[:],
+                    start=True,
+                    stop=True,
+                )
+                nc.scalar.copy(y[:, b], sums[:])
+            return y
+
+        def scatter(e, y):
+            slots = slice(C * e, C * (e + 1))
+            places = slots_list[:, C // LIST_ROWS * e : C // LIST_ROWS * (e + 1)]
+            for b in range(OUT_TILES):
+                nc.vector.tensor_tensor(windows[b][:].indirect(places), y[:, b], gate_sb[:, b, slots], MULT)
+
+        quantise_x(0)
+        gather_words(0)
+        quantise_x(1)
+        y = None
+        for e in range(E):
+            quantise_w1(e)
+            if e == 0:
+                gather_words(1)
+                gather_scales()
+            else:
+                scatter(e - 1, y)
+            h_words, h_scales = layer1(e)
+            if e % 2 == 0:
+                quantise_w2(e // 2)
+            y = layer2(e, h_words, h_scales)
+        scatter(E - 1, y)
+
+        for b in range(OUT_TILES):
+            nc.sync.dma_start(out[P * b : P * (b + 1), :], windows[b][:])

from contextlib import ExitStack

import concourse.mybir as mybir

K, T, E, C, H, N = 1024, 1536, 4, 256, 512, 256
FLOPS = 2 * E * C * (K * H + H * N)

F32 = mybir.dt.float32
BF16 = mybir.dt.bfloat16
U32 = mybir.dt.uint32
U16 = mybir.dt.uint16
U8 = mybir.dt.uint8
FP8X4 = mybir.dt.float8_e4m3fn_x4
MULT = mybir.AluOpType.mult
RELU = mybir.ActivationFunctionType.Relu
SQUARE = mybir.ActivationFunctionType.Square

P = 128
PACK = 4
PASSES = K // (P * PACK)
TILES = H // P
BANK_TILES = 2
OUT_TILES = N // P
LIST_ROWS = 16
CHUNK = 512

X_VECTOR = 192
W1_VECTOR = (0, 64, 32, 48)


def interleave(copy, grouped, raw):
    copy(
        grouped.rearrange("p (c i) j -> p c j i", i=4),
        raw.rearrange("p j (c i) -> p c j i", i=4),
    )


def interleave_w1(copy, grouped, raw, first, last):
    copy(
        grouped.rearrange("p (t m) j -> p m j t", t=TILES)[:, first:last],
        raw.rearrange("p j (m t) -> p m j t", t=TILES)[:, first:last],
    )


def tile_routed_moe_kernel(tc, xT, w1, w2, gate, offs, out):
    nc = tc.nc
    with ExitStack() as ctx:
        keep = ctx.enter_context(tc.tile_pool(name="keep", bufs=1))
        raw_pool = ctx.enter_context(tc.tile_pool(name="raw_pool", bufs=11))
        x_pool = ctx.enter_context(tc.tile_pool(name="x_pool", bufs=2))
        w1_pool = ctx.enter_context(tc.tile_pool(name="w1_pool", bufs=2))
        w2_pool = ctx.enter_context(tc.tile_pool(name="w2_pool", bufs=2))
        relu_pool = ctx.enter_context(tc.tile_pool(name="relu_pool", bufs=2))
        h_pool = ctx.enter_context(tc.tile_pool(name="h_pool", bufs=2))
        h_codes_pool = ctx.enter_context(tc.tile_pool(name="h_codes_pool", bufs=3))
        y_pool = ctx.enter_context(tc.tile_pool(name="y_pool", bufs=2))
        h_psum = ctx.enter_context(tc.psum_pool(name="h_psum", bufs=5))
        y_psum = ctx.enter_context(tc.psum_pool(name="y_psum", bufs=3))

        slots_list = keep.tile([P, E * C // LIST_ROWS], U16, name="slots_list", align_bytes=64)
        words = [keep.tile([P, T], U32, name=f"words{a}", align_bytes=64) for a in range(PASSES)]
        scales = keep.tile([P, T], U8, name="scales", align_bytes=64)
        nc.gpsimd.memset(scales[:], 0)
        windows = [keep.tile([P, T], F32, name=f"window{b}", align_bytes=64) for b in range(OUT_TILES)]
        slot_words = keep.tile([P, PASSES, E * C], U32, name="slot_words", align_bytes=64)
        slot_scales = keep.tile([P, E * C], U8, name="slot_scales", align_bytes=64)
        gate_sb = keep.tile([P, OUT_TILES, E * C], F32, name="gate_sb", align_bytes=64)
        w2_words = keep.tile([P, E, N], U32, name="w2_words", align_bytes=64)
        w2_scales = keep.tile([P, E, N], U8, name="w2_scales", align_bytes=64)

        x_raw, w1_raw, w2_raw, w1_words, w1_scales = {}, {}, {}, {}, {}

        def load_x(a):
            rows = xT.rearrange("(a p j) n -> a p j n", p=P, j=PACK)[a]
            for c in range(T // CHUNK):
                x_raw[a, c] = raw_pool.tile([P, PACK, CHUNK], F32, name="raw", align_bytes=64)
                nc.sync.dma_start(x_raw[a, c][:], rows[:, :, c * CHUNK : (c + 1) * CHUNK])

        def load_w1(e):
            for a in range(PASSES):
                w1_raw[e, a] = raw_pool.tile([P, PACK, H], F32, name="raw", align_bytes=64)
                nc.sync.dma_start(w1_raw[e, a][:], w1[e].rearrange("(a p j) h -> a p j h", p=P, j=PACK)[a])

        def load_w2(pair):
            w2_raw[pair] = keep.tile([P, 2, PACK, N], F32, name=f"w2_raw{pair}", align_bytes=64)
            for i in range(2):
                nc.sync.dma_start(w2_raw[pair][:, i], w2[2 * pair + i].rearrange("(p j) n -> p j n", j=PACK))

        nc.sync.dma_start(slots_list[:], offs)
        load_x(0)
        load_x(1)
        load_w1(0)
        load_w2(0)
        load_w1(1)
        load_w1(2)
        nc.sync.dma_start(gate_sb[:], gate.rearrange("(b p) j -> p b j", p=P))
        load_w1(3)
        load_w2(1)

        for b in range(OUT_TILES):
            nc.vector.memset(windows[b][:], 0.0)

        def quantise_x(a):
            for c in range(T // CHUNK):
                grouped = x_pool.tile([P, CHUNK, PACK], BF16, name="x_grouped", align_bytes=64)
                raw = x_raw[a, c]
                interleave(nc.vector.tensor_copy, grouped[:, :X_VECTOR], raw[:, :, :X_VECTOR])
                interleave(nc.scalar.copy, grouped[:, X_VECTOR:], raw[:, :, X_VECTOR:])
                tokens = slice(c * CHUNK, (c + 1) * CHUNK)
                nc.vector.quantize_mx(
                    out=words[a][:, tokens].bitcast(FP8X4),
                    scales=scales[4 * a : P, tokens],
                    in_=grouped[:].rearrange("p c j -> p (c j)"),
                )

        def gather_words(a):
            nc.vector.tensor_copy(slot_words[:, a, :], words[a][:].indirect(slots_list[:]))

        def gather_scales():
            nc.vector.tensor_copy(slot_scales[:], scales[:].indirect(slots_list[:]))

        def quantise_w1(e):
            w1_words[e] = keep.tile([P, PASSES, H], U32, name=f"w1_words{e}", align_bytes=64)
            w1_scales[e] = keep.tile([P, PASSES, H], U8, name=f"w1_scales{e}", align_bytes=64)
            at_once = PASSES if e == 0 else 1
            vector = W1_VECTOR[e]
            for a0 in range(0, PASSES, at_once):
                grouped = w1_pool.tile([P, at_once, H, PACK], BF16, name="w1_grouped", align_bytes=64)
                for i in range(at_once):
                    raw = w1_raw[e, a0 + i][:]
                    if vector > 0:
                        interleave_w1(nc.vector.tensor_copy, grouped[:, i], raw, 0, vector)
                    interleave_w1(nc.scalar.copy, grouped[:, i], raw, vector, P)
                nc.vector.quantize_mx(
                    out=w1_words[e][:, a0 : a0 + at_once].rearrange("p a h -> p (a h)").bitcast(FP8X4),
                    scales=w1_scales[e][:, a0 : a0 + at_once].rearrange("p a h -> p (a h)"),
                    in_=grouped[:].rearrange("p a h j -> p (a h j)"),
                )

        def quantise_w2(pair):
            grouped = w2_pool.tile([P, 2, N, PACK], BF16, name="w2_grouped", align_bytes=64)
            for i in range(2):
                interleave(nc.scalar.copy, grouped[:, i], w2_raw[pair][:, i])
            experts = slice(2 * pair, 2 * pair + 2)
            nc.vector.quantize_mx(
                out=w2_words[:, experts].rearrange("p e n -> p (e n)").bitcast(FP8X4),
                scales=w2_scales[:, experts].rearrange("p e n -> p (e n)"),
                in_=grouped[:].rearrange("p e n j -> p (e n j)"),
            )

        def layer1(e):
            slots = slice(C * e, C * (e + 1))
            relu = relu_pool.tile([P, TILES // BANK_TILES, C, BANK_TILES], F32, name="relu", align_bytes=64)
            for u in range(TILES // BANK_TILES):
                sums = h_psum.tile([P, BANK_TILES, C], F32, name="h_sums")
                for i in range(BANK_TILES):
                    t = BANK_TILES * u + i
                    columns = slice(P * t, P * (t + 1))
                    for a in range(PASSES):
                        nc.tensor.matmul_mx(
                            out=sums[:, i],
                            lhsT=w1_words[e][:, a, columns].bitcast(FP8X4),
                            lhsT_scale=w1_scales[e][:, a, columns],
                            rhs=slot_words[:, a, slots].bitcast(FP8X4),
                            rhs_scale=slot_scales[4 * a : P, slots],
                            start=(a == 0),
                            stop=(a == PASSES - 1),
                        )
                nc.scalar.activation(relu[:, u], sums[:].rearrange("p i n -> p n i"), RELU)

            grouped = h_pool.tile([P, C, PACK], BF16, name="h_grouped", align_bytes=64)

            def views(first, last):
                return (
                    grouped[:, first:last].rearrange("p n (u i) -> p n u i", u=TILES // BANK_TILES),
                    relu[:, :, first:last].rearrange("p u n i -> p n u i"),
                )

            scalar_slots = C // 2 if e in (0, E - 1) else C
            squared, source = views(0, scalar_slots)
            nc.scalar.activation(squared, source, SQUARE)
            if scalar_slots < C:
                squared, source = views(scalar_slots, C)
                nc.vector.tensor_tensor(squared, source, source, MULT)

            h_words = h_codes_pool.tile([P, C], U32, name="h_words", align_bytes=64)
            h_scales = h_codes_pool.tile([P, C], U8, name="h_scales", align_bytes=64)
            nc.vector.quantize_mx(
                out=h_words[:].bitcast(FP8X4), scales=h_scales[:], in_=grouped[:].rearrange("p n j -> p (n j)")
            )
            return h_words, h_scales

        def layer2(e, h_words, h_scales):
            y = y_pool.tile([P, OUT_TILES, C], F32, name="y", align_bytes=64)
            for b in range(OUT_TILES):
                features = slice(P * b, P * (b + 1))
                sums = y_psum.tile([P, C], F32, name="y_sums")
                nc.tensor.matmul_mx(
                    out=sums[:],
                    lhsT=w2_words[:, e, features].bitcast(FP8X4),
                    lhsT_scale=w2_scales[:, e, features],
                    rhs=h_words[:].bitcast(FP8X4),
                    rhs_scale=h_scales[:],
                    start=True,
                    stop=True,
                )
                nc.scalar.copy(y[:, b], sums[:])
            return y

        def scatter(e, y):
            slots = slice(C * e, C * (e + 1))
            places = slots_list[:, C // LIST_ROWS * e : C // LIST_ROWS * (e + 1)]
            for b in range(OUT_TILES):
                nc.vector.tensor_tensor(windows[b][:].indirect(places), y[:, b], gate_sb[:, b, slots], MULT)

        quantise_x(0)
        gather_words(0)
        quantise_x(1)
        y = None
        for e in range(E):
            quantise_w1(e)
            if e == 0:
                gather_words(1)
                gather_scales()
            else:
                scatter(e - 1, y)
            h_words, h_scales = layer1(e)
            if e % 2 == 0:
                quantise_w2(e // 2)
            y = layer2(e, h_words, h_scales)
        scatter(E - 1, y)

        for b in range(OUT_TILES):
            nc.sync.dma_start(out[P * b : P * (b + 1), :], windows[b][:])
